import numpy as np
CORES = [0,8,64,72]
N = 4
def setup_inputs(rng):
    return {"x": rng.standard_normal((N, 32, 512), dtype=np.float32)}
def reference(x):
    s = x.sum(axis=0, dtype=np.float64).astype(x.dtype)
    return {"y": np.broadcast_to(s, (N,) + s.shape)}

@@ -1,0 +1,52 @@
+import concourse.bass as bass
+from concourse.mybir import AluOpType
+
+SCRATCH = {
+    "xs": ("sbuf", [128, 128], "float32"),
+    "lp": ("sbuf", [128, 128], "float32"),
+    "lf": ("sbuf", [128, 128], "float32"),
+    "ha": ("sbuf", [128, 128], "float32"),
+    "hb": ("sbuf", [128, 128], "float32"),
+}
+SEMAPHORES = ["loaded", "stored", "sent", "arrived", "peer", "fold"]
+
+HELPER = 2
+
+
+def rank_program(g, core, T, topo):
+    chips = [topo.chip(c) for c in T.cores]
+    chip = topo.chip(core)
+    if chip not in chips:
+        return
+    peer_chip = [c for c in chips if topo.same_plane(c, chip)][0]
+    mate_chip = [c for c in chips if topo.mates(c, chip)][0]
+    rank_on = {topo.chip(c): c for c in T.cores}
+    S = T.sem
+
+    def send(dst, out, src, sem, mask):
+        rid, pid, _se = topo.addr(dst)
+        g.remote_dma(out, src, sem, S.sent, pid, rid, mask)
+
+    if T.rank_of(core) is not None:
+        g.dma_start(T.xs[:], T.x[:]).then_inc(S.loaded, 16)
+        g.dma_start(T.y[:], T.x[:]).then_inc(S.stored, 16)
+        g.wait_ge(S.loaded, 16)
+        send(peer_chip * 8 + HELPER, T.hb[:], T.xs[:], S.arrived, 0x00FF)
+        send(chip * 8 + HELPER, T.ha[:], T.xs[:], S.arrived, 0xFFFF)
+        send(rank_on[peer_chip], T.lp[:], T.xs[:], S.peer, 0x00FF)
+        g.wait_ge(S.peer, 8)
+        g.wait_ge(S.stored, 16)
+        g.dma_start(T.y[:], T.lp[:], accum_op=AluOpType.add).then_inc(S.stored, 16)
+        g.wait_ge(S.fold, 8)
+        g.wait_ge(S.stored, 32)
+        g.dma_start(T.y[:], T.lf[:], accum_op=AluOpType.add).then_inc(S.stored, 16)
+        g.wait_ge(S.stored, 48)
+        g.wait_ge(S.sent, 32)
+    elif core % 8 == HELPER:
+        rid, pid, _se = topo.addr(rank_on[mate_chip])
+        g.wait_ge(S.arrived, 24)
+        g.remote_dma_fused(
+            [bass.RemoteDMATransfer(dst_ids=[bass.DstId(rid=rid, pnc=pid)], dma_engine_mask=0x00FF,
+                                    remote_sem=S.fold, srcs=[T.ha[:], T.hb[:]], dsts=[T.lf[:]], alu_op=1)],
+            local_sem=S.sent)
+        g.wait_ge(S.sent, 8)

@@ -2,11 +2,11 @@ import concourse.bass as bass
 from concourse.mybir import AluOpType
 
 SCRATCH = {
-    "xs": ("sbuf", [128, 128], "float32"),
-    "lp": ("sbuf", [128, 128], "float32"),
-    "lf": ("sbuf", [128, 128], "float32"),
-    "ha": ("sbuf", [128, 128], "float32"),
-    "hb": ("sbuf", [128, 128], "float32"),
+    "xs": ("dram", [128, 128], "float32"),
+    "lp": ("dram", [128, 128], "float32"),
+    "lf": ("dram", [128, 128], "float32"),
+    "ha": ("dram", [128, 128], "float32"),
+    "hb": ("dram", [128, 128], "float32"),
 }
 SEMAPHORES = ["loaded", "stored", "sent", "arrived", "peer", "fold"]
 
@@ -36,10 +36,10 @@ def rank_program(g, core, T, topo):
         send(rank_on[peer_chip], T.lp[:], T.xs[:], S.peer, 0x00FF)
         g.wait_ge(S.peer, 8)
         g.wait_ge(S.stored, 16)
-        g.dma_start(T.y[:], T.lp[:], accum_op=AluOpType.add).then_inc(S.stored, 16)
+        g.dma_start(T.y[:], T.lp[:], accum_op=AluOpType.add, max_dma_last_dim=8192).then_inc(S.stored, 16)
         g.wait_ge(S.fold, 8)
         g.wait_ge(S.stored, 32)
-        g.dma_start(T.y[:], T.lf[:], accum_op=AluOpType.add).then_inc(S.stored, 16)
+        g.dma_start(T.y[:], T.lf[:], accum_op=AluOpType.add, max_dma_last_dim=8192).then_inc(S.stored, 16)
         g.wait_ge(S.stored, 48)
         g.wait_ge(S.sent, 32)
     elif core % 8 == HELPER:

@@ -1,16 +1,19 @@
 import concourse.bass as bass
 from concourse.mybir import AluOpType
 
+HELPERS = [2, 6, 3, 7]
+K = len(HELPERS)
+W = 128 // K
+E = 8 // K
+
 SCRATCH = {
-    "xs": ("dram", [128, 128], "float32"),
-    "lp": ("dram", [128, 128], "float32"),
-    "lf": ("dram", [128, 128], "float32"),
-    "ha": ("dram", [128, 128], "float32"),
-    "hb": ("dram", [128, 128], "float32"),
+    "xs": ("dram", [K, 128, W], "float32"),
+    "lp": ("dram", [K, 128, W], "float32"),
+    "lf": ("dram", [K, 128, W], "float32"),
+    "ha": ("dram", [128, W], "float32"),
+    "hb": ("dram", [128, W], "float32"),
 }
 SEMAPHORES = ["loaded", "stored", "sent", "arrived", "peer", "fold"]
-
-HELPER = 2
 
 
 def rank_program(g, core, T, topo):
@@ -23,30 +26,35 @@ def rank_program(g, core, T, topo):
     rank_on = {topo.chip(c): c for c in T.cores}
     S = T.sem
 
-    def send(dst, out, src, sem, mask):
+    def xfer(dst, out, srcs, sem, mask):
         rid, pid, _se = topo.addr(dst)
-        g.remote_dma(out, src, sem, S.sent, pid, rid, mask)
+        return bass.RemoteDMATransfer(dst_ids=[bass.DstId(rid=rid, pnc=pid)], dma_engine_mask=mask, remote_sem=sem,
+                                      srcs=srcs, dsts=[out], alu_op=1 if len(srcs) > 1 else 0)
+
+    def engines(k, base):
+        return ((1 << E) - 1) << (base + k * E)
 
     if T.rank_of(core) is not None:
         g.dma_start(T.xs[:], T.x[:]).then_inc(S.loaded, 16)
         g.dma_start(T.y[:], T.x[:]).then_inc(S.stored, 16)
         g.wait_ge(S.loaded, 16)
-        send(peer_chip * 8 + HELPER, T.hb[:], T.xs[:], S.arrived, 0x00FF)
-        send(chip * 8 + HELPER, T.ha[:], T.xs[:], S.arrived, 0xFFFF)
-        send(rank_on[peer_chip], T.lp[:], T.xs[:], S.peer, 0x00FF)
+        g.remote_dma_fused(
+            [xfer(peer_chip * 8 + h, T.hb[:], [T.xs[k]], S.arrived, engines(k, 0)) for k, h in enumerate(HELPERS)]
+            + [xfer(chip * 8 + h, T.ha[:], [T.xs[k]], S.arrived, engines(k, 8)) for k, h in enumerate(HELPERS)],
+            local_sem=S.sent)
+        g.remote_dma_fused(
+            [xfer(rank_on[peer_chip], T.lp[k], [T.xs[k]], S.peer, engines(k, 0)) for k in range(K)],
+            local_sem=S.sent)
         g.wait_ge(S.peer, 8)
         g.wait_ge(S.stored, 16)
         g.dma_start(T.y[:], T.lp[:], accum_op=AluOpType.add, max_dma_last_dim=8192).then_inc(S.stored, 16)
-        g.wait_ge(S.fold, 8)
+        g.wait_ge(S.fold, 8 * K)
         g.wait_ge(S.stored, 32)
         g.dma_start(T.y[:], T.lf[:], accum_op=AluOpType.add, max_dma_last_dim=8192).then_inc(S.stored, 16)
         g.wait_ge(S.stored, 48)
-        g.wait_ge(S.sent, 32)
-    elif core % 8 == HELPER:
-        rid, pid, _se = topo.addr(rank_on[mate_chip])
-        g.wait_ge(S.arrived, 24)
-        g.remote_dma_fused(
-            [bass.RemoteDMATransfer(dst_ids=[bass.DstId(rid=rid, pnc=pid)], dma_engine_mask=0x00FF,
-                                    remote_sem=S.fold, srcs=[T.ha[:], T.hb[:]], dsts=[T.lf[:]], alu_op=1)],
-            local_sem=S.sent)
+        g.wait_ge(S.sent, 24)
+    elif core % 8 in HELPERS:
+        k = HELPERS.index(core % 8)
+        g.wait_ge(S.arrived, 2 * E)
+        g.remote_dma_fused([xfer(rank_on[mate_chip], T.lf[k], [T.ha[:], T.hb[:]], S.fold, 0x00FF)], local_sem=S.sent)
         g.wait_ge(S.sent, 8)

@@ -8,12 +8,13 @@ E = 8 // K
 
 SCRATCH = {
     "xs": ("dram", [K, 128, W], "float32"),
-    "lp": ("dram", [K, 128, W], "float32"),
+    "xw": ("dram", [128, 128], "float32"),
+    "lp": ("dram", [128, 128], "float32"),
     "lf": ("dram", [K, 128, W], "float32"),
     "ha": ("dram", [128, W], "float32"),
     "hb": ("dram", [128, W], "float32"),
 }
-SEMAPHORES = ["loaded", "stored", "sent", "arrived", "peer", "fold"]
+SEMAPHORES = ["loaded", "loadedw", "stored", "sent", "arrived", "peer", "fold"]
 
 
 def rank_program(g, core, T, topo):
@@ -36,14 +37,16 @@ def rank_program(g, core, T, topo):
 
     if T.rank_of(core) is not None:
         g.dma_start(T.xs[:], T.x[:]).then_inc(S.loaded, 16)
+        g.dma_start(T.xw[:], T.x[:]).then_inc(S.loadedw, 16)
         g.dma_start(T.y[:], T.x[:]).then_inc(S.stored, 16)
         g.wait_ge(S.loaded, 16)
         g.remote_dma_fused(
-            [xfer(peer_chip * 8 + h, T.hb[:], [T.xs[k]], S.arrived, engines(k, 0)) for k, h in enumerate(HELPERS)]
-            + [xfer(chip * 8 + h, T.ha[:], [T.xs[k]], S.arrived, engines(k, 8)) for k, h in enumerate(HELPERS)],
+            [xfer(peer_chip * 8 + h, T.hb[:], [T.xs[k]], S.arrived, engines(k, 0)) for k, h in enumerate(HELPERS)],
             local_sem=S.sent)
+        g.wait_ge(S.loadedw, 16)
+        g.remote_dma_fused([xfer(rank_on[peer_chip], T.lp[:], [T.xw[:]], S.peer, 0x00FF)], local_sem=S.sent)
         g.remote_dma_fused(
-            [xfer(rank_on[peer_chip], T.lp[k], [T.xs[k]], S.peer, engines(k, 0)) for k in range(K)],
+            [xfer(chip * 8 + h, T.ha[:], [T.xs[k]], S.arrived, engines(k, 8)) for k, h in enumerate(HELPERS)],
             local_sem=S.sent)
         g.wait_ge(S.peer, 8)
         g.wait_ge(S.stored, 16)

import concourse.bass as bass
from concourse.mybir import AluOpType

HELPERS = [2, 6, 3, 7]
K = len(HELPERS)
W = 128 // K
E = 8 // K

SCRATCH = {
    "xs": ("dram", [K, 128, W], "float32"),
    "xw": ("dram", [128, 128], "float32"),
    "lp": ("dram", [128, 128], "float32"),
    "lf": ("dram", [K, 128, W], "float32"),
    "ha": ("dram", [128, W], "float32"),
    "hb": ("dram", [128, W], "float32"),
}
SEMAPHORES = ["loaded", "loadedw", "stored", "sent", "arrived", "peer", "fold"]


def rank_program(g, core, T, topo):
    chips = [topo.chip(c) for c in T.cores]
    chip = topo.chip(core)
    if chip not in chips:
        return
    peer_chip = [c for c in chips if topo.same_plane(c, chip)][0]
    mate_chip = [c for c in chips if topo.mates(c, chip)][0]
    rank_on = {topo.chip(c): c for c in T.cores}
    S = T.sem

    def xfer(dst, out, srcs, sem, mask):
        rid, pid, _se = topo.addr(dst)
        return bass.RemoteDMATransfer(dst_ids=[bass.DstId(rid=rid, pnc=pid)], dma_engine_mask=mask, remote_sem=sem,
                                      srcs=srcs, dsts=[out], alu_op=1 if len(srcs) > 1 else 0)

    def engines(k, base):
        return ((1 << E) - 1) << (base + k * E)

    if T.rank_of(core) is not None:
        g.dma_start(T.xs[:], T.x[:]).then_inc(S.loaded, 16)
        g.dma_start(T.xw[:], T.x[:]).then_inc(S.loadedw, 16)
        g.dma_start(T.y[:], T.x[:]).then_inc(S.stored, 16)
        g.wait_ge(S.loaded, 16)
        g.remote_dma_fused(
            [xfer(peer_chip * 8 + h, T.hb[:], [T.xs[k]], S.arrived, engines(k, 0)) for k, h in enumerate(HELPERS)],
            local_sem=S.sent)
        g.wait_ge(S.loadedw, 16)
        g.remote_dma_fused([xfer(rank_on[peer_chip], T.lp[:], [T.xw[:]], S.peer, 0x00FF)], local_sem=S.sent)
        g.remote_dma_fused(
            [xfer(chip * 8 + h, T.ha[:], [T.xs[k]], S.arrived, engines(k, 8)) for k, h in enumerate(HELPERS)],
            local_sem=S.sent)
        g.wait_ge(S.peer, 8)
        g.wait_ge(S.stored, 16)
        g.dma_start(T.y[:], T.lp[:], accum_op=AluOpType.add, max_dma_last_dim=8192).then_inc(S.stored, 16)
        g.wait_ge(S.fold, 8 * K)
        g.wait_ge(S.stored, 32)
        g.dma_start(T.y[:], T.lf[:], accum_op=AluOpType.add, max_dma_last_dim=8192).then_inc(S.stored, 16)
        g.wait_ge(S.stored, 48)
        g.wait_ge(S.sent, 24)
    elif core % 8 in HELPERS:
        k = HELPERS.index(core % 8)
        g.wait_ge(S.arrived, 2 * E)
        g.remote_dma_fused([xfer(rank_on[mate_chip], T.lf[k], [T.ha[:], T.hb[:]], S.fold, 0x00FF)], local_sem=S.sent)
        g.wait_ge(S.sent, 8)
